import numpy as np
import ml_dtypes


def mxq(x, axis, fmt="e4m3"):
    dtype, down = {"e4m3": (ml_dtypes.float8_e4m3fn, 7), "e5m2": (ml_dtypes.float8_e5m2, 14)}[fmt]
    v = np.moveaxis(np.asarray(x, np.float32).astype(ml_dtypes.bfloat16).astype(np.float64), axis, -1)
    blocks = v.reshape(v.shape[:-1] + (-1, 32))
    amax = np.abs(blocks).max(-1, keepdims=True)
    byte = np.maximum(np.where(amax > 0, np.frexp(amax)[1] - 1 + 127, 0) - down, 1)
    scale = np.exp2(byte - 127.0)
    codes = (blocks / scale).astype(np.float32).astype(dtype).astype(np.float64)
    return np.moveaxis((codes * scale).reshape(v.shape), -1, axis)


WIDE = False


def mx_kscale(k):
    if not WIDE:
        return np.ones(k)
    levels = np.array([10, -10, 5, -5, 0])
    if k % 512:
        return np.exp2(np.random.permutation(np.resize(levels, k // 32))).repeat(32)
    a = np.empty((k // 512, 16))
    for p in range(k // 512):
        a[p, :8] = np.random.permutation(np.resize(levels, 8))
        for g in range(8):
            far = levels[np.abs(levels - a[p, g]) >= 10]
            a[p, g + 8] = far[np.random.randint(len(far))]
    return np.exp2(a.ravel()).repeat(32)


def f64(x):
    return np.asarray(x).astype(np.float64)


def striped(idx):
    return np.tile(idx.reshape(-1, 16).T, (8, 1)).astype(np.uint16)


def unstriped(offs):
    return offs[:16].T.reshape(-1).astype(np.int64)


E2M1 = np.array([0.0, 0.5, 1.0, 1.5, 2.0, 3.0, 4.0, 6.0, -0.0, -0.5, -1.0, -1.5, -2.0, -3.0, -4.0, -6.0])


def pack_weight(w, fmt):
    k, n = w.shape
    w = f64(np.asarray(w, np.float32).astype(ml_dtypes.bfloat16)).reshape(k // 32, 32, n)
    amax = np.abs(w).max(1)
    if fmt == "e4m3":
        byte = np.frexp(amax)[1] - 1 + 127 - 7
    else:
        mant, ex = np.frexp(amax / 6.0)
        byte = np.where(mant > 0.5, ex, ex - 1) + 127
    byte = np.clip(np.where(amax > 0, byte, 1), 1, 254)
    scaled = (w * np.exp2(127.0 - byte)[:, None, :]).reshape(k, n).astype(np.float32)
    by_word = np.ascontiguousarray(scaled.reshape(k // 512, 128, 4, n).transpose(0, 1, 3, 2))
    if fmt == "e4m3":
        words = by_word.astype(ml_dtypes.float8_e4m3fn).view(np.uint8)
    else:
        c = by_word.astype(ml_dtypes.float4_e2m1fn).view(np.uint8) & 0xF
        words = (c[..., 0::2] | (c[..., 1::2] << 4)).reshape(k // 512, 128, 2 * n)
    return np.ascontiguousarray(words), np.ascontiguousarray(byte.astype(np.uint8).reshape(k // 512, 16, n))


def unpack_weight(words, scales, fmt):
    g, _, n = scales.shape
    words = np.ascontiguousarray(words).reshape(g, 128, n, -1)
    if fmt == "e4m3":
        vals = words.view(ml_dtypes.float8_e4m3fn).astype(np.float64)
    else:
        nib = np.empty((g, 128, n, 4), np.uint8)
        nib[..., 0::2] = words & 0xF
        nib[..., 1::2] = words >> 4
        vals = E2M1[nib]
    vals = vals * np.repeat(np.exp2(scales.astype(np.float64) - 127.0), 8, axis=1)[..., None]
    return vals.transpose(0, 1, 3, 2).reshape(g * 512, n)


def sigmoid(v):
    return 1.0 / (1.0 + np.exp(-np.maximum(v, -700.0)))


K, T, E, C, H, N = 512, 512, 8, 128, 512, 384
R = 2


def by_expert(wq, xq):
    return np.concatenate([wq[e].T @ xq[:, e * C:(e + 1) * C] for e in range(E)], axis=1)


def setup_inputs():
    n = np.random.standard_normal
    s = mx_kscale(K)[:, None]
    u = mx_kscale(H)
    slot_token = np.concatenate([r * (T // R) + np.random.permutation(T // R)[:C // R] for e in range(E) for r in range(R)])
    w1 = [pack_weight(m, "e2m1") for m in n((E, K, H)) / np.sqrt(K) / s[None]]
    w3 = [pack_weight(m, "e2m1") for m in n((E, K, H)) / np.sqrt(K) / s[None] * u[None, None, :]]
    w2 = [pack_weight(m, "e2m1") for m in n((E, H, N)) / np.sqrt(H) / u[None, :, None]]
    return {
        "xT": (n((K, T)) * s).astype(np.float32),
        "w1_words": np.stack([m[0] for m in w1]),
        "w1_scales": np.stack([m[1] for m in w1]),
        "w3_words": np.stack([m[0] for m in w3]),
        "w3_scales": np.stack([m[1] for m in w3]),
        "w2_words": np.stack([m[0] for m in w2]),
        "w2_scales": np.stack([m[1] for m in w2]),
        "offs": striped(slot_token),
    }


def reference(xT, w1_words, w1_scales, w3_words, w3_scales, w2_words, w2_scales, offs):
    idx = unstriped(offs)
    w1 = np.stack([unpack_weight(w1_words[e], w1_scales[e], "e2m1") for e in range(E)])
    w3 = np.stack([unpack_weight(w3_words[e], w3_scales[e], "e2m1") for e in range(E)])
    w2 = np.stack([unpack_weight(w2_words[e], w2_scales[e], "e2m1") for e in range(E)])
    xq = mxq(f64(xT)[:, idx], 0, "e4m3")
    h = sigmoid(by_expert(w1, xq))
    h = h * by_expert(w3, xq)
    y = by_expert(w2, mxq(h, 0, "e4m3"))
    return y.reshape(N, E, R, C // R).transpose(0, 2, 1, 3).reshape(N, E * C)

@@ -1,0 +1,201 @@
+from contextlib import ExitStack
+
+import concourse.mybir as mybir
+from concourse.masks import make_identity
+
+P = 128
+PACK = 4
+K, T, E, C, H, N = 512, 512, 8, 128, 512, 384
+R = 2
+SLOTS = E * C
+N_TILES = N // P
+FLOPS = 2 * SLOTS * (2 * K * H + H * N)
+
+F32 = mybir.dt.float32
+BF16 = mybir.dt.bfloat16
+I32 = mybir.dt.int32
+U32 = mybir.dt.uint32
+U16 = mybir.dt.uint16
+U8 = mybir.dt.uint8
+FP8X4 = mybir.dt.float8_e4m3fn_x4
+FP4X4 = mybir.dt.float4_e2m1fn_x4
+MULT = mybir.AluOpType.mult
+SIGMOID = mybir.ActivationFunctionType.Sigmoid
+
+X_CHUNK = 256
+VECTOR_TOKENS = 176
+
+
+def tile_moe_eps_glu_sigmoid_kernel(
+    tc, xT, w1_words, w1_scales, w3_words, w3_scales, w2_words, w2_scales, offs, out
+):
+    nc = tc.nc
+    with ExitStack() as ctx:
+        keep = ctx.enter_context(tc.tile_pool(name="keep", bufs=1))
+        work = ctx.enter_context(tc.tile_pool(name="work", bufs=3))
+        psum = ctx.enter_context(tc.psum_pool(name="psum", bufs=2))
+
+        offsets = keep.tile([P, SLOTS // 16], U16, name="offsets")
+        x_raw = [keep.tile([P, PACK, X_CHUNK], F32, name=f"x_raw{c}") for c in range(T // X_CHUNK)]
+        x_grouped = keep.tile([P, T, PACK], BF16, name="x_grouped", align_bytes=64)
+        x_codes = keep.tile([P, T], U32, name="x_codes", align_bytes=64)
+        x_scales = keep.tile([P, T], U8, name="x_scales", align_bytes=64)
+        s_codes = keep.tile([P, SLOTS], U32, name="s_codes", align_bytes=64)
+        s_scales = keep.tile([P, SLOTS], U8, name="s_scales", align_bytes=64)
+        w1 = keep.tile([P, E, 2 * H], U8, name="w1", align_bytes=64)
+        w3 = keep.tile([P, E, 2 * H], U8, name="w3", align_bytes=64)
+        w2 = keep.tile([P, E, 2 * N], U8, name="w2", align_bytes=64)
+        w1_sc = keep.tile([P, E, H], U8, name="w1_sc", align_bytes=64)
+        w3_sc = keep.tile([P, E, H], U8, name="w3_sc", align_bytes=64)
+        w2_sc = keep.tile([P, E, N], U8, name="w2_sc", align_bytes=64)
+        ident = keep.tile([P, P], F32, name="ident")
+        warm = keep.tile([P, 8], F32, name="warm")
+        warm_out = keep.tile([P, 8], F32, name="warm_out")
+
+        for c in range(T // X_CHUNK):
+            nc.sync.dma_start(
+                out=x_raw[c][:],
+                in_=xT[:, c * X_CHUNK : (c + 1) * X_CHUNK].rearrange("(p j) w -> p j w", j=PACK),
+            )
+        nc.sync.dma_start(offsets[:], offs)
+
+        nc.vector.memset(warm[:], 0.0)
+        nc.scalar.activation(warm_out[:], warm[:], SIGMOID)
+        nc.vector.memset(w1_sc[:].bitcast(I32), 0)
+        nc.vector.memset(w3_sc[:].bitcast(I32), 0)
+        nc.vector.memset(w2_sc[:].bitcast(I32), 0)
+        nc.gpsimd.memset(x_scales[:], 0)
+
+        def load_words(engine, tile, words, first, last):
+            engine.dma_start(
+                out=tile[:, first:last, :].bitcast(I32),
+                in_=words[first:last].bitcast(I32).rearrange("e s p w -> p (e s) w"),
+            )
+
+        def load_scales(tile, scales):
+            rows = scales.bitcast(I32).rearrange("e s (q r) w -> r q (e s) w", r=4)
+            for r in range(4):
+                nc.sync.dma_start(out=tile[:].bitcast(I32)[r:P:32], in_=rows[r])
+
+        load_words(nc.gpsimd, w1, w1_words, 0, 2)
+        load_words(nc.gpsimd, w3, w3_words, 0, 2)
+        make_identity(nc, ident[:])
+        load_scales(w1_sc, w1_scales)
+        load_scales(w3_sc, w3_scales)
+        load_words(nc.sync, w2, w2_words, 0, 4)
+        load_scales(w2_sc, w2_scales)
+        load_words(nc.sync, w1, w1_words, 2, 5)
+        load_words(nc.sync, w3, w3_words, 2, 5)
+        load_words(nc.sync, w1, w1_words, 5, 8)
+        load_words(nc.sync, w3, w3_words, 5, 8)
+        load_words(nc.sync, w2, w2_words, 4, 8)
+
+        for c in range(T // X_CHUNK):
+            lo, mid, hi = c * X_CHUNK, c * X_CHUNK + VECTOR_TOKENS, (c + 1) * X_CHUNK
+            nc.scalar.copy(
+                out=x_grouped[:, mid:hi, :],
+                in_=x_raw[c][:, :, VECTOR_TOKENS:].rearrange("p j w -> p w j"),
+            )
+            nc.vector.tensor_copy(
+                out=x_grouped[:, lo:mid, :],
+                in_=x_raw[c][:, :, :VECTOR_TOKENS].rearrange("p j w -> p w j"),
+            )
+            nc.vector.quantize_mx(
+                out=x_codes[:, lo:hi].bitcast(FP8X4),
+                scales=x_scales[:, lo:hi],
+                in_=x_grouped[:, lo:hi, :].rearrange("p w j -> p (w j)"),
+            )
+
+        def gather(first, last):
+            cols = slice(first * C, last * C)
+            entries = offsets[:, first * C // 16 : last * C // 16]
+            nc.vector.tensor_copy(out=s_codes[:, cols], in_=x_codes[:].indirect(entries))
+            nc.vector.tensor_copy(out=s_scales[:, cols], in_=x_scales[:].indirect(entries))
+
+        a_bank, b_bank, h_tile, turned, h_q, y_bank = {}, {}, {}, {}, {}, {}
+
+        def first_layer(e):
+            cols = slice(e * C, (e + 1) * C)
+            a_bank[e] = psum.tile([P, H], F32, name="a")
+            b_bank[e] = psum.tile([P, H], F32, name="b")
+            for bank, w, sc in ((a_bank[e], w1, w1_sc), (b_bank[e], w3, w3_sc)):
+                nc.tensor.matmul_mx(
+                    out=bank[:],
+                    lhsT=s_codes[:, cols].bitcast(FP8X4),
+                    lhsT_scale=s_scales[:, cols],
+                    rhs=w[:, e, :].bitcast(FP4X4),
+                    rhs_scale=sc[:, e, :],
+                    start=True,
+                    stop=True,
+                )
+
+        def gate(e):
+            sig = work.tile([P, 2, P, 2], F32, name="sig")
+            nc.scalar.activation(sig[:], a_bank[e][:].rearrange("p (q u d) -> p u q d", u=2, d=2), SIGMOID)
+            h = work.tile([P, 2, P, 2], BF16, name="h")
+            nc.vector.tensor_tensor(
+                h[:], b_bank[e][:].rearrange("p (q u d) -> p u q d", u=2, d=2), sig[:], MULT
+            )
+            h_tile[e] = h
+
+        def turn(e):
+            words = h_tile[e][:].rearrange("p u q d -> p (u q d)").bitcast(F32)
+            turned[e] = psum.tile([P, 2, P], F32, name="turn")
+            for u in range(2):
+                nc.tensor.transpose(turned[e][:, u, :], words[:, u * P : (u + 1) * P], ident[:])
+
+        def second_layer(e):
+            hT = work.tile([P, C * PACK], BF16, name="hT", align_bytes=64)
+            nc.scalar.copy(
+                out=hT[:].bitcast(F32).rearrange("p (c u) -> p c u", u=2),
+                in_=turned[e][:].rearrange("p u c -> p c u"),
+            )
+            codes = work.tile([P, C], U32, name="h_codes", align_bytes=64)
+            scales = work.tile([P, C], U8, name="h_scales", align_bytes=64)
+            nc.vector.quantize_mx(out=codes[:].bitcast(FP8X4), scales=scales[:], in_=hT[:])
+            y_bank[e] = psum.tile([P, N_TILES, C], F32, name="y")
+            for m in range(N_TILES):
+                nc.tensor.matmul_mx(
+                    out=y_bank[e][:, m, :],
+                    lhsT=w2[:, e, 2 * P * m : 2 * P * (m + 1)].bitcast(FP4X4),
+                    lhsT_scale=w2_sc[:, e, P * m : P * (m + 1)],
+                    rhs=codes[:].bitcast(FP8X4),
+                    rhs_scale=scales[:],
+                    start=True,
+                    stop=True,
+                )
+
+        GROUP = 2
+        staged = {}
+
+        def finish(e):
+            if e % GROUP == 0:
+                staged[e // GROUP] = work.tile([P, N_TILES, R, GROUP, C // R], F32, name="staged")
+            tile = staged[e // GROUP]
+            nc.scalar.copy(
+                out=tile[:, :, :, e % GROUP, :],
+                in_=y_bank[e][:].rearrange("p m (r u) -> p m r u", r=R),
+            )
+            if e % GROUP == GROUP - 1:
+                width = C // R
+                for r in range(R):
+                    lo = r * (SLOTS // R) + (e - GROUP + 1) * width
+                    nc.sync.dma_start(
+                        out=out[:, lo : lo + GROUP * width].rearrange("(m p) w -> p m w", p=P),
+                        in_=tile[:, :, r, :, :].rearrange("p m g u -> p m (g u)"),
+                    )
+
+        gather(0, 1)
+        first_layer(0)
+        gather(1, 2)
+        first_layer(1)
+        for e in range(E):
+            gate(e)
+            if e + 2 < E:
+                gather(e + 2, e + 3)
+                first_layer(e + 2)
+            turn(e)
+            second_layer(e)
+            if e >= 1:
+                finish(e - 1)
+        finish(E - 1)

@@ -33,6 +33,7 @@ def tile_moe_eps_glu_sigmoid_kernel(
     with ExitStack() as ctx:
         keep = ctx.enter_context(tc.tile_pool(name="keep", bufs=1))
         work = ctx.enter_context(tc.tile_pool(name="work", bufs=3))
+        sigs = ctx.enter_context(tc.tile_pool(name="sigs", bufs=8))
         psum = ctx.enter_context(tc.psum_pool(name="psum", bufs=2))
 
         offsets = keep.tile([P, SLOTS // 16], U16, name="offsets")
@@ -42,9 +43,6 @@ def tile_moe_eps_glu_sigmoid_kernel(
         x_scales = keep.tile([P, T], U8, name="x_scales", align_bytes=64)
         s_codes = keep.tile([P, SLOTS], U32, name="s_codes", align_bytes=64)
         s_scales = keep.tile([P, SLOTS], U8, name="s_scales", align_bytes=64)
-        w1 = keep.tile([P, E, 2 * H], U8, name="w1", align_bytes=64)
-        w3 = keep.tile([P, E, 2 * H], U8, name="w3", align_bytes=64)
-        w2 = keep.tile([P, E, 2 * N], U8, name="w2", align_bytes=64)
         w1_sc = keep.tile([P, E, H], U8, name="w1_sc", align_bytes=64)
         w3_sc = keep.tile([P, E, H], U8, name="w3_sc", align_bytes=64)
         w2_sc = keep.tile([P, E, N], U8, name="w2_sc", align_bytes=64)
@@ -52,12 +50,12 @@ def tile_moe_eps_glu_sigmoid_kernel(
         warm = keep.tile([P, 8], F32, name="warm")
         warm_out = keep.tile([P, 8], F32, name="warm_out")
 
+        nc.sync.dma_start(offsets[:], offs)
         for c in range(T // X_CHUNK):
             nc.sync.dma_start(
                 out=x_raw[c][:],
                 in_=xT[:, c * X_CHUNK : (c + 1) * X_CHUNK].rearrange("(p j) w -> p j w", j=PACK),
             )
-        nc.sync.dma_start(offsets[:], offs)
 
         nc.vector.memset(warm[:], 0.0)
         nc.scalar.activation(warm_out[:], warm[:], SIGMOID)
@@ -65,30 +63,32 @@ def tile_moe_eps_glu_sigmoid_kernel(
         nc.vector.memset(w3_sc[:].bitcast(I32), 0)
         nc.vector.memset(w2_sc[:].bitcast(I32), 0)
         nc.gpsimd.memset(x_scales[:], 0)
+        make_identity(nc, ident[:])
 
-        def load_words(engine, tile, words, first, last):
-            engine.dma_start(
-                out=tile[:, first:last, :].bitcast(I32),
+        def load_words(name, words, first, last):
+            tile = keep.tile([P, last - first, words.shape[3]], U8, name=f"{name}_{first}", align_bytes=64)
+            nc.sync.dma_start(
+                out=tile[:].bitcast(I32),
                 in_=words[first:last].bitcast(I32).rearrange("e s p w -> p (e s) w"),
             )
+            return {e: tile[:, e - first, :] for e in range(first, last)}
 
         def load_scales(tile, scales):
             rows = scales.bitcast(I32).rearrange("e s (q r) w -> r q (e s) w", r=4)
             for r in range(4):
                 nc.sync.dma_start(out=tile[:].bitcast(I32)[r:P:32], in_=rows[r])
 
-        load_words(nc.gpsimd, w1, w1_words, 0, 2)
-        load_words(nc.gpsimd, w3, w3_words, 0, 2)
-        make_identity(nc, ident[:])
+        w1, w3, w2 = {}, {}, {}
         load_scales(w1_sc, w1_scales)
+        w1.update(load_words("w1", w1_words, 0, 2))
+        w1.update(load_words("w1", w1_words, 2, 5))
+        w3.update(load_words("w3", w3_words, 0, 4))
         load_scales(w3_sc, w3_scales)
-        load_words(nc.sync, w2, w2_words, 0, 4)
+        w1.update(load_words("w1", w1_words, 5, 8))
         load_scales(w2_sc, w2_scales)
-        load_words(nc.sync, w1, w1_words, 2, 5)
-        load_words(nc.sync, w3, w3_words, 2, 5)
-        load_words(nc.sync, w1, w1_words, 5, 8)
-        load_words(nc.sync, w3, w3_words, 5, 8)
-        load_words(nc.sync, w2, w2_words, 4, 8)
+        w3.update(load_words("w3", w3_words, 4, 8))
+        w2.update(load_words("w2", w2_words, 0, 4))
+        w2.update(load_words("w2", w2_words, 4, 8))
 
         for c in range(T // X_CHUNK):
             lo, mid, hi = c * X_CHUNK, c * X_CHUNK + VECTOR_TOKENS, (c + 1) * X_CHUNK
@@ -106,96 +106,131 @@ def tile_moe_eps_glu_sigmoid_kernel(
                 in_=x_grouped[:, lo:hi, :].rearrange("p w j -> p (w j)"),
             )
 
-        def gather(first, last):
-            cols = slice(first * C, last * C)
-            entries = offsets[:, first * C // 16 : last * C // 16]
+        a_bank, b_bank, sig_tile, h_tile, y_bank = {}, {}, {}, {}, {}
+
+        def project(e, name, w, sc):
+            cols = slice(e * C, (e + 1) * C)
+            bank = psum.tile([P, H], F32, name=name)
+            nc.tensor.matmul_mx(
+                out=bank[:],
+                lhsT=s_codes[:, cols].bitcast(FP8X4),
+                lhsT_scale=s_scales[:, cols],
+                rhs=w[e].bitcast(FP4X4),
+                rhs_scale=sc[:, e, :],
+                start=True,
+                stop=True,
+            )
+            return bank
+
+        def front(e):
+            cols = slice(e * C, (e + 1) * C)
+            entries = offsets[:, e * C // 16 : (e + 1) * C // 16]
             nc.vector.tensor_copy(out=s_codes[:, cols], in_=x_codes[:].indirect(entries))
             nc.vector.tensor_copy(out=s_scales[:, cols], in_=x_scales[:].indirect(entries))
+            a = project(e, "a", w1, w1_sc)
+            sig_tile[e] = sigs.tile([P, 2, P, 2], F32, name="sig")
+            nc.scalar.activation(sig_tile[e][:], a[:].rearrange("p (q u d) -> p u q d", u=2, d=2), SIGMOID)
 
-        a_bank, b_bank, h_tile, turned, h_q, y_bank = {}, {}, {}, {}, {}, {}
+        def linear(e):
+            if e not in b_bank:
+                b_bank[e] = project(e, "b", w3, w3_sc)
 
-        def first_layer(e):
-            cols = slice(e * C, (e + 1) * C)
-            a_bank[e] = psum.tile([P, H], F32, name="a")
-            b_bank[e] = psum.tile([P, H], F32, name="b")
-            for bank, w, sc in ((a_bank[e], w1, w1_sc), (b_bank[e], w3, w3_sc)):
-                nc.tensor.matmul_mx(
-                    out=bank[:],
-                    lhsT=s_codes[:, cols].bitcast(FP8X4),
-                    lhsT_scale=s_scales[:, cols],
-                    rhs=w[:, e, :].bitcast(FP4X4),
-                    rhs_scale=sc[:, e, :],
-                    start=True,
-                    stop=True,
-                )
-
-        def gate(e):
-            sig = work.tile([P, 2, P, 2], F32, name="sig")
-            nc.scalar.activation(sig[:], a_bank[e][:].rearrange("p (q u d) -> p u q d", u=2, d=2), SIGMOID)
+        def gate(e, pieces):
             h = work.tile([P, 2, P, 2], BF16, name="h")
-            nc.vector.tensor_tensor(
-                h[:], b_bank[e][:].rearrange("p (q u d) -> p u q d", u=2, d=2), sig[:], MULT
-            )
+            b = b_bank[e][:].rearrange("p (q u d) -> p u q d", u=2, d=2)
+            for u in range(0, 2, 2 // pieces):
+                part = slice(u, u + 2 // pieces)
+                nc.vector.tensor_tensor(h[:, part], b[:, part], sig_tile[e][:, part], MULT)
             h_tile[e] = h
 
-        def turn(e):
-            words = h_tile[e][:].rearrange("p u q d -> p (u q d)").bitcast(F32)
-            turned[e] = psum.tile([P, 2, P], F32, name="turn")
-            for u in range(2):
-                nc.tensor.transpose(turned[e][:, u, :], words[:, u * P : (u + 1) * P], ident[:])
+        def turn(group):
+            bank = psum.tile([P, len(group), 2, P], F32, name="turn")
+            for i, e in enumerate(group):
+                words = h_tile[e][:].rearrange("p u q d -> p (u q d)").bitcast(F32)
+                for u in range(2):
+                    nc.tensor.transpose(bank[:, i, u, :], words[:, u * P : (u + 1) * P], ident[:])
+            return bank
 
-        def second_layer(e):
-            hT = work.tile([P, C * PACK], BF16, name="hT", align_bytes=64)
-            nc.scalar.copy(
-                out=hT[:].bitcast(F32).rearrange("p (c u) -> p c u", u=2),
-                in_=turned[e][:].rearrange("p u c -> p c u"),
-            )
-            codes = work.tile([P, C], U32, name="h_codes", align_bytes=64)
-            scales = work.tile([P, C], U8, name="h_scales", align_bytes=64)
+        def second_layer(group, bank, last):
+            n = len(group)
+            hT = work.tile([P, n * C * PACK], BF16, name="hT", align_bytes=64)
+            dst = hT[:].bitcast(F32).rearrange("p (g c u) -> p g c u", g=n, u=2)
+            src = bank[:].rearrange("p g u c -> p g c u")
+            if last:
+                nc.vector.tensor_copy(out=dst, in_=src)
+            else:
+                nc.scalar.copy(out=dst, in_=src)
+            codes = work.tile([P, n * C], U32, name="h_codes", align_bytes=64)
+            scales = work.tile([P, n * C], U8, name="h_scales", align_bytes=64)
             nc.vector.quantize_mx(out=codes[:].bitcast(FP8X4), scales=scales[:], in_=hT[:])
-            y_bank[e] = psum.tile([P, N_TILES, C], F32, name="y")
-            for m in range(N_TILES):
-                nc.tensor.matmul_mx(
-                    out=y_bank[e][:, m, :],
-                    lhsT=w2[:, e, 2 * P * m : 2 * P * (m + 1)].bitcast(FP4X4),
-                    lhsT_scale=w2_sc[:, e, P * m : P * (m + 1)],
-                    rhs=codes[:].bitcast(FP8X4),
-                    rhs_scale=scales[:],
-                    start=True,
-                    stop=True,
-                )
+            for i, e in enumerate(group):
+                y_bank[e] = []
+                for tiles in ((0, 1), (2,)) if e == E - 1 else ((0, 1, 2),):
+                    y = psum.tile([P, len(tiles), C], F32, name="y")
+                    for j, m in enumerate(tiles):
+                        nc.tensor.matmul_mx(
+                            out=y[:, j, :],
+                            lhsT=w2[e][:, 2 * P * m : 2 * P * (m + 1)].bitcast(FP4X4),
+                            lhsT_scale=w2_sc[:, e, P * m : P * (m + 1)],
+                            rhs=codes[:, i * C : (i + 1) * C].bitcast(FP8X4),
+                            rhs_scale=scales[:, i * C : (i + 1) * C],
+                            start=True,
+                            stop=True,
+                        )
+                    y_bank[e].append((tiles, y))
 
-        GROUP = 2
+        width = C // R
+        STORES = [(0, 1, 2, 3), (4, 5), (6,)]
         staged = {}
 
         def finish(e):
-            if e % GROUP == 0:
-                staged[e // GROUP] = work.tile([P, N_TILES, R, GROUP, C // R], F32, name="staged")
-            tile = staged[e // GROUP]
-            nc.scalar.copy(
-                out=tile[:, :, :, e % GROUP, :],
-                in_=y_bank[e][:].rearrange("p m (r u) -> p m r u", r=R),
-            )
-            if e % GROUP == GROUP - 1:
-                width = C // R
-                for r in range(R):
-                    lo = r * (SLOTS // R) + (e - GROUP + 1) * width
-                    nc.sync.dma_start(
-                        out=out[:, lo : lo + GROUP * width].rearrange("(m p) w -> p m w", p=P),
-                        in_=tile[:, :, r, :, :].rearrange("p m g u -> p m (g u)"),
-                    )
+            for tiles, bank in y_bank[e]:
+                y = bank[:].rearrange("p m (r u) -> p m r u", r=R)
+                if e == E - 1:
+                    part = keep.tile([P, len(tiles), R, width], F32, name=f"part{tiles[0]}")
+                    if len(tiles) == 1:
+                        nc.vector.tensor_copy(out=part[:], in_=y)
+                    else:
+                        nc.scalar.copy(out=part[:], in_=y)
+                    for j, m in enumerate(tiles):
+                        nc.sync.dma_start(
+                            out=out[m * P : (m + 1) * P, :]
+                            .rearrange("p (r s) -> p r s", r=R)[:, :, e * width : (e + 1) * width],
+                            in_=part[:, j],
+                        )
+                    continue
+                store = [s for s in STORES if e in s][0]
+                if e == store[0]:
+                    staged[store] = keep.tile([P, N_TILES, R, len(store), width], F32, name=f"staged{e}")
+                nc.scalar.copy(out=staged[store][:, :, :, e - store[0], :], in_=y)
+                if e == store[-1]:
+                    for r in range(R):
+                        lo = r * (SLOTS // R) + store[0] * width
+                        nc.sync.dma_start(
+                            out=out[:, lo : lo + len(store) * width].rearrange("(m p) w -> p m w", p=P),
+                            in_=staged[store][:, :, r, :, :].rearrange("p m g u -> p m (g u)"),
+                        )
 
-        gather(0, 1)
-        first_layer(0)
-        gather(1, 2)
-        first_layer(1)
-        for e in range(E):
-            gate(e)
-            if e + 2 < E:
-                gather(e + 2, e + 3)
-                first_layer(e + 2)
-            turn(e)
-            second_layer(e)
-            if e >= 1:
-                finish(e - 1)
-        finish(E - 1)
+        GROUPS = [(0, 1), (2, 3), (4, 5), (6,), (7,)]
+        AHEAD = 6
+        LATE = 2
+        for e in range(AHEAD):
+            front(e)
+        upcoming = AHEAD
+        for i in range(len(GROUPS) + LATE):
+            if i < len(GROUPS):
+                group = GROUPS[i]
+                for e in group:
+                    linear(e)
+                for e in group:
+                    gate(e, 2 if e == E - 1 else 1)
+                for e in GROUPS[i + 1] if i + 1 < len(GROUPS) else ():
+                    linear(e)
+                second_layer(group, turn(group), group[-1] == E - 1)
+                for e in group:
+                    if upcoming < E:
+                        front(upcoming)
+                        upcoming += 1
+            if i >= LATE:
+                for e in GROUPS[i - LATE]:
+                    finish(e)

from contextlib import ExitStack

import concourse.mybir as mybir
from concourse.masks import make_identity

P = 128
PACK = 4
K, T, E, C, H, N = 512, 512, 8, 128, 512, 384
R = 2
SLOTS = E * C
N_TILES = N // P
FLOPS = 2 * SLOTS * (2 * K * H + H * N)

F32 = mybir.dt.float32
BF16 = mybir.dt.bfloat16
I32 = mybir.dt.int32
U32 = mybir.dt.uint32
U16 = mybir.dt.uint16
U8 = mybir.dt.uint8
FP8X4 = mybir.dt.float8_e4m3fn_x4
FP4X4 = mybir.dt.float4_e2m1fn_x4
MULT = mybir.AluOpType.mult
SIGMOID = mybir.ActivationFunctionType.Sigmoid

X_CHUNK = 256
VECTOR_TOKENS = 176


def tile_moe_eps_glu_sigmoid_kernel(
    tc, xT, w1_words, w1_scales, w3_words, w3_scales, w2_words, w2_scales, offs, out
):
    nc = tc.nc
    with ExitStack() as ctx:
        keep = ctx.enter_context(tc.tile_pool(name="keep", bufs=1))
        work = ctx.enter_context(tc.tile_pool(name="work", bufs=3))
        sigs = ctx.enter_context(tc.tile_pool(name="sigs", bufs=8))
        psum = ctx.enter_context(tc.psum_pool(name="psum", bufs=2))

        offsets = keep.tile([P, SLOTS // 16], U16, name="offsets")
        x_raw = [keep.tile([P, PACK, X_CHUNK], F32, name=f"x_raw{c}") for c in range(T // X_CHUNK)]
        x_grouped = keep.tile([P, T, PACK], BF16, name="x_grouped", align_bytes=64)
        x_codes = keep.tile([P, T], U32, name="x_codes", align_bytes=64)
        x_scales = keep.tile([P, T], U8, name="x_scales", align_bytes=64)
        s_codes = keep.tile([P, SLOTS], U32, name="s_codes", align_bytes=64)
        s_scales = keep.tile([P, SLOTS], U8, name="s_scales", align_bytes=64)
        w1_sc = keep.tile([P, E, H], U8, name="w1_sc", align_bytes=64)
        w3_sc = keep.tile([P, E, H], U8, name="w3_sc", align_bytes=64)
        w2_sc = keep.tile([P, E, N], U8, name="w2_sc", align_bytes=64)
        ident = keep.tile([P, P], F32, name="ident")
        warm = keep.tile([P, 8], F32, name="warm")
        warm_out = keep.tile([P, 8], F32, name="warm_out")

        nc.sync.dma_start(offsets[:], offs)
        for c in range(T // X_CHUNK):
            nc.sync.dma_start(
                out=x_raw[c][:],
                in_=xT[:, c * X_CHUNK : (c + 1) * X_CHUNK].rearrange("(p j) w -> p j w", j=PACK),
            )

        nc.vector.memset(warm[:], 0.0)
        nc.scalar.activation(warm_out[:], warm[:], SIGMOID)
        nc.vector.memset(w1_sc[:].bitcast(I32), 0)
        nc.vector.memset(w3_sc[:].bitcast(I32), 0)
        nc.vector.memset(w2_sc[:].bitcast(I32), 0)
        nc.gpsimd.memset(x_scales[:], 0)
        make_identity(nc, ident[:])

        def load_words(name, words, first, last):
            tile = keep.tile([P, last - first, words.shape[3]], U8, name=f"{name}_{first}", align_bytes=64)
            nc.sync.dma_start(
                out=tile[:].bitcast(I32),
                in_=words[first:last].bitcast(I32).rearrange("e s p w -> p (e s) w"),
            )
            return {e: tile[:, e - first, :] for e in range(first, last)}

        def load_scales(tile, scales):
            rows = scales.bitcast(I32).rearrange("e s (q r) w -> r q (e s) w", r=4)
            for r in range(4):
                nc.sync.dma_start(out=tile[:].bitcast(I32)[r:P:32], in_=rows[r])

        w1, w3, w2 = {}, {}, {}
        load_scales(w1_sc, w1_scales)
        w1.update(load_words("w1", w1_words, 0, 2))
        w1.update(load_words("w1", w1_words, 2, 5))
        w3.update(load_words("w3", w3_words, 0, 4))
        load_scales(w3_sc, w3_scales)
        w1.update(load_words("w1", w1_words, 5, 8))
        load_scales(w2_sc, w2_scales)
        w3.update(load_words("w3", w3_words, 4, 8))
        w2.update(load_words("w2", w2_words, 0, 4))
        w2.update(load_words("w2", w2_words, 4, 8))

        for c in range(T // X_CHUNK):
            lo, mid, hi = c * X_CHUNK, c * X_CHUNK + VECTOR_TOKENS, (c + 1) * X_CHUNK
            nc.scalar.copy(
                out=x_grouped[:, mid:hi, :],
                in_=x_raw[c][:, :, VECTOR_TOKENS:].rearrange("p j w -> p w j"),
            )
            nc.vector.tensor_copy(
                out=x_grouped[:, lo:mid, :],
                in_=x_raw[c][:, :, :VECTOR_TOKENS].rearrange("p j w -> p w j"),
            )
            nc.vector.quantize_mx(
                out=x_codes[:, lo:hi].bitcast(FP8X4),
                scales=x_scales[:, lo:hi],
                in_=x_grouped[:, lo:hi, :].rearrange("p w j -> p (w j)"),
            )

        a_bank, b_bank, sig_tile, h_tile, y_bank = {}, {}, {}, {}, {}

        def project(e, name, w, sc):
            cols = slice(e * C, (e + 1) * C)
            bank = psum.tile([P, H], F32, name=name)
            nc.tensor.matmul_mx(
                out=bank[:],
                lhsT=s_codes[:, cols].bitcast(FP8X4),
                lhsT_scale=s_scales[:, cols],
                rhs=w[e].bitcast(FP4X4),
                rhs_scale=sc[:, e, :],
                start=True,
                stop=True,
            )
            return bank

        def front(e):
            cols = slice(e * C, (e + 1) * C)
            entries = offsets[:, e * C // 16 : (e + 1) * C // 16]
            nc.vector.tensor_copy(out=s_codes[:, cols], in_=x_codes[:].indirect(entries))
            nc.vector.tensor_copy(out=s_scales[:, cols], in_=x_scales[:].indirect(entries))
            a = project(e, "a", w1, w1_sc)
            sig_tile[e] = sigs.tile([P, 2, P, 2], F32, name="sig")
            nc.scalar.activation(sig_tile[e][:], a[:].rearrange("p (q u d) -> p u q d", u=2, d=2), SIGMOID)

        def linear(e):
            if e not in b_bank:
                b_bank[e] = project(e, "b", w3, w3_sc)

        def gate(e, pieces):
            h = work.tile([P, 2, P, 2], BF16, name="h")
            b = b_bank[e][:].rearrange("p (q u d) -> p u q d", u=2, d=2)
            for u in range(0, 2, 2 // pieces):
                part = slice(u, u + 2 // pieces)
                nc.vector.tensor_tensor(h[:, part], b[:, part], sig_tile[e][:, part], MULT)
            h_tile[e] = h

        def turn(group):
            bank = psum.tile([P, len(group), 2, P], F32, name="turn")
            for i, e in enumerate(group):
                words = h_tile[e][:].rearrange("p u q d -> p (u q d)").bitcast(F32)
                for u in range(2):
                    nc.tensor.transpose(bank[:, i, u, :], words[:, u * P : (u + 1) * P], ident[:])
            return bank

        def second_layer(group, bank, last):
            n = len(group)
            hT = work.tile([P, n * C * PACK], BF16, name="hT", align_bytes=64)
            dst = hT[:].bitcast(F32).rearrange("p (g c u) -> p g c u", g=n, u=2)
            src = bank[:].rearrange("p g u c -> p g c u")
            if last:
                nc.vector.tensor_copy(out=dst, in_=src)
            else:
                nc.scalar.copy(out=dst, in_=src)
            codes = work.tile([P, n * C], U32, name="h_codes", align_bytes=64)
            scales = work.tile([P, n * C], U8, name="h_scales", align_bytes=64)
            nc.vector.quantize_mx(out=codes[:].bitcast(FP8X4), scales=scales[:], in_=hT[:])
            for i, e in enumerate(group):
                y_bank[e] = []
                for tiles in ((0, 1), (2,)) if e == E - 1 else ((0, 1, 2),):
                    y = psum.tile([P, len(tiles), C], F32, name="y")
                    for j, m in enumerate(tiles):
                        nc.tensor.matmul_mx(
                            out=y[:, j, :],
                            lhsT=w2[e][:, 2 * P * m : 2 * P * (m + 1)].bitcast(FP4X4),
                            lhsT_scale=w2_sc[:, e, P * m : P * (m + 1)],
                            rhs=codes[:, i * C : (i + 1) * C].bitcast(FP8X4),
                            rhs_scale=scales[:, i * C : (i + 1) * C],
                            start=True,
                            stop=True,
                        )
                    y_bank[e].append((tiles, y))

        width = C // R
        STORES = [(0, 1, 2, 3), (4, 5), (6,)]
        staged = {}

        def finish(e):
            for tiles, bank in y_bank[e]:
                y = bank[:].rearrange("p m (r u) -> p m r u", r=R)
                if e == E - 1:
                    part = keep.tile([P, len(tiles), R, width], F32, name=f"part{tiles[0]}")
                    if len(tiles) == 1:
                        nc.vector.tensor_copy(out=part[:], in_=y)
                    else:
                        nc.scalar.copy(out=part[:], in_=y)
                    for j, m in enumerate(tiles):
                        nc.sync.dma_start(
                            out=out[m * P : (m + 1) * P, :]
                            .rearrange("p (r s) -> p r s", r=R)[:, :, e * width : (e + 1) * width],
                            in_=part[:, j],
                        )
                    continue
                store = [s for s in STORES if e in s][0]
                if e == store[0]:
                    staged[store] = keep.tile([P, N_TILES, R, len(store), width], F32, name=f"staged{e}")
                nc.scalar.copy(out=staged[store][:, :, :, e - store[0], :], in_=y)
                if e == store[-1]:
                    for r in range(R):
                        lo = r * (SLOTS // R) + store[0] * width
                        nc.sync.dma_start(
                            out=out[:, lo : lo + len(store) * width].rearrange("(m p) w -> p m w", p=P),
                            in_=staged[store][:, :, r, :, :].rearrange("p m g u -> p m (g u)"),
                        )

        GROUPS = [(0, 1), (2, 3), (4, 5), (6,), (7,)]
        AHEAD = 6
        LATE = 2
        for e in range(AHEAD):
            front(e)
        upcoming = AHEAD
        for i in range(len(GROUPS) + LATE):
            if i < len(GROUPS):
                group = GROUPS[i]
                for e in group:
                    linear(e)
                for e in group:
                    gate(e, 2 if e == E - 1 else 1)
                for e in GROUPS[i + 1] if i + 1 < len(GROUPS) else ():
                    linear(e)
                second_layer(group, turn(group), group[-1] == E - 1)
                for e in group:
                    if upcoming < E:
                        front(upcoming)
                        upcoming += 1
            if i >= LATE:
                for e in GROUPS[i - LATE]:
                    finish(e)
